import numpy as np
import ml_dtypes


def mxq(x, axis, fmt="e4m3"):
    dtype, down = {"e4m3": (ml_dtypes.float8_e4m3fn, 7), "e5m2": (ml_dtypes.float8_e5m2, 14)}[fmt]
    v = np.moveaxis(np.asarray(x, np.float32).astype(ml_dtypes.bfloat16).astype(np.float64), axis, -1)
    blocks = v.reshape(v.shape[:-1] + (-1, 32))
    amax = np.abs(blocks).max(-1, keepdims=True)
    byte = np.maximum(np.where(amax > 0, np.frexp(amax)[1] - 1 + 127, 0) - down, 1)
    scale = np.exp2(byte - 127.0)
    codes = (blocks / scale).astype(np.float32).astype(dtype).astype(np.float64)
    return np.moveaxis((codes * scale).reshape(v.shape), -1, axis)


WIDE = False


def mx_kscale(k):
    if not WIDE:
        return np.ones(k)
    levels = np.array([10, -10, 5, -5, 0])
    if k % 512:
        return np.exp2(np.random.permutation(np.resize(levels, k // 32))).repeat(32)
    a = np.empty((k // 512, 16))
    for p in range(k // 512):
        a[p, :8] = np.random.permutation(np.resize(levels, 8))
        for g in range(8):
            far = levels[np.abs(levels - a[p, g]) >= 10]
            a[p, g + 8] = far[np.random.randint(len(far))]
    return np.exp2(a.ravel()).repeat(32)


def f64(x):
    return np.asarray(x).astype(np.float64)


def striped(idx):
    return np.tile(np.asarray(idx).reshape(-1, 16).T, (8, 1)).astype(np.uint16)


def unstriped(offs):
    return offs[:16].T.reshape(-1).astype(np.int64)


E2M1 = np.array([0.0, 0.5, 1.0, 1.5, 2.0, 3.0, 4.0, 6.0, -0.0, -0.5, -1.0, -1.5, -2.0, -3.0, -4.0, -6.0])


def pack_weight(w, fmt):
    k, n = w.shape
    w = f64(np.asarray(w, np.float32).astype(ml_dtypes.bfloat16)).reshape(k // 32, 32, n)
    amax = np.abs(w).max(1)
    if fmt == "e4m3":
        byte = np.frexp(amax)[1] - 1 + 127 - 7
    else:
        mant, ex = np.frexp(amax / 6.0)
        byte = np.where(mant > 0.5, ex, ex - 1) + 127
    byte = np.clip(np.where(amax > 0, byte, 1), 1, 254)
    scaled = (w * np.exp2(127.0 - byte)[:, None, :]).reshape(k, n).astype(np.float32)
    by_word = np.ascontiguousarray(scaled.reshape(k // 512, 128, 4, n).transpose(0, 1, 3, 2))
    if fmt == "e4m3":
        words = by_word.astype(ml_dtypes.float8_e4m3fn).view(np.uint8)
    else:
        c = by_word.astype(ml_dtypes.float4_e2m1fn).view(np.uint8) & 0xF
        words = (c[..., 0::2] | (c[..., 1::2] << 4)).reshape(k // 512, 128, 2 * n)
    return np.ascontiguousarray(words), np.ascontiguousarray(byte.astype(np.uint8).reshape(k // 512, 16, n))


def unpack_weight(words, scales, fmt):
    g, _, n = scales.shape
    words = np.ascontiguousarray(words).reshape(g, 128, n, -1)
    if fmt == "e4m3":
        vals = words.view(ml_dtypes.float8_e4m3fn).astype(np.float64)
    else:
        nib = np.empty((g, 128, n, 4), np.uint8)
        nib[..., 0::2] = words & 0xF
        nib[..., 1::2] = words >> 4
        vals = E2M1[nib]
    vals = vals * np.repeat(np.exp2(scales.astype(np.float64) - 127.0), 8, axis=1)[..., None]
    return vals.transpose(0, 1, 3, 2).reshape(g * 512, n)


def bf(x):
    return np.asarray(x, np.float32).astype(ml_dtypes.bfloat16)


def planes(Y):
    r, m = Y.shape
    b = f64(bf(Y)).reshape(r // 32, 32, m)
    amax = np.abs(b).max(1)
    byte = np.clip(np.where(amax > 0, np.frexp(amax)[1] - 1 + 127 - 7, 1), 1, 254)
    codes = (b * np.exp2(127.0 - byte)[:, None, :]).reshape(r, m).astype(np.float32).astype(ml_dtypes.float8_e4m3fn).view(np.uint8)
    words = codes.reshape(r // 512, 128, 4, m).transpose(0, 1, 3, 2)
    return np.ascontiguousarray(words), np.ascontiguousarray(byte.astype(np.uint8).reshape(r // 512, 16, m))


K, L, T, J, N = 1024, 512, 1024, 512, 512


def setup_inputs():
    n = np.random.standard_normal
    idx = np.random.permutation(T)[:J]
    fk = mx_kscale(K)
    fl = mx_kscale(L)
    xtp = pack_weight(n((K, T)) / fk[:, None], "e2m1")
    xep = pack_weight(n((L, J)) / fl[:, None], "e4m3")
    wep = pack_weight(n((L, N)) * 1 / np.sqrt(L) * fl[:, None], "e2m1")
    return {
        "xt_words": xtp[0],
        "xt_scales": xtp[1],
        "ws": (n((K, N)) * 1 / np.sqrt(K) * fk[:, None]).astype(np.float32),
        "xe_words": xep[0],
        "xe_scales": xep[1],
        "we_words": wep[0],
        "we_scales": wep[1],
        "res": (1.0 * n((N, T))).astype(np.float32),
        "offs": striped(idx),
    }


def reference(xt_words, xt_scales, ws, xe_words, xe_scales, we_words, we_scales, res, offs):
    idx = unstriped(offs)
    xtu = unpack_weight(xt_words, xt_scales, "e2m1")
    xeu = unpack_weight(xe_words, xe_scales, "e4m3")
    weu = unpack_weight(we_words, we_scales, "e2m1")
    wsq = mxq(f64(ws), 0, "e4m3")
    u = wsq.T @ xtu
    p = weu.T @ xeu
    d = np.tanh(p) * u[:, idx]
    dp = np.zeros((N, T))
    dp[:, idx] = d
    y = u - dp + 0.2 * f64(res)
    words, scales = planes(y)
    return y, words, scales

@@ -1,0 +1,314 @@
+from contextlib import ExitStack
+
+import concourse.mybir as mybir
+from concourse.masks import make_identity
+
+K, L, T, J, N = 1024, 512, 1024, 512, 512
+FLOPS = 2 * K * N * T + 2 * L * N * J
+
+F32 = mybir.dt.float32
+BF16 = mybir.dt.bfloat16
+I32 = mybir.dt.int32
+U32 = mybir.dt.uint32
+U16 = mybir.dt.uint16
+U8 = mybir.dt.uint8
+FP8X4 = mybir.dt.float8_e4m3fn_x4
+FP4X4 = mybir.dt.float4_e2m1fn_x4
+ACT = mybir.ActivationFunctionType
+ALU = mybir.AluOpType
+
+P = 128
+R = 4
+BANK = 512
+HALVES = T // BANK
+QUART = 256
+RES_W = 0.2
+UP = 5.0
+
+
+def tile_moe_expert_scales_shared_answer_pl_kernel(
+    tc, xt_words, xt_scales, ws, xe_words, xe_scales, we_words, we_scales, res, offs, out_0, out_1, out_2
+):
+    nc = tc.nc
+    with ExitStack() as ctx:
+        held = ctx.enter_context(tc.tile_pool(name="held", bufs=1))
+        ring = ctx.enter_context(tc.tile_pool(name="ring", bufs=2))
+        psum = ctx.enter_context(tc.psum_pool(name="psum", bufs=1))
+
+        def bank(b, name):
+            return psum.tile([P, BANK], F32, name=name, tag="bank%d" % b)
+
+        offsets = held.tile([P, J // 16], U16, name="offsets")
+
+        xt_sc = held.tile([P, 2 * T], U8, name="xt_sc", align_bytes=64)
+        xe_sc = held.tile([P, J], U8, name="xe_sc", align_bytes=64)
+        we_sc_raw = held.tile([P, N], U8, name="we_sc_raw", align_bytes=64)
+        nc.vector.memset(xt_sc[:].bitcast(I32), 0)
+        nc.vector.memset(we_sc_raw[:].bitcast(I32), 0)
+        nc.vector.memset(xe_sc[:].bitcast(I32), 0)
+
+        ident = held.tile([P, P], F32, name="ident")
+        make_identity(nc, ident[:])
+        we_raw = held.tile([P, 2 * N], U8, name="we_raw", align_bytes=64)
+        ws_v = ws.rearrange("(g p j) n -> g p j n", g=2, j=4)
+        ws_raw = {}
+        xt_w = held.tile([P, 2 * 2 * T], U8, name="xt_w", align_bytes=64)
+
+        def load_ws(g, h):
+            ws_raw[g, h] = ring.tile([P, 4, N // 2], F32, name="ws_raw%d%d" % (g, h), tag="stage")
+            nc.sync.dma_start(out=ws_raw[g, h][:], in_=ws_v[g][:, :, h * (N // 2) : (h + 1) * (N // 2)])
+
+        load_ws(0, 0)
+        xts = xt_scales.rearrange("g (q i) c -> i q g c", i=4)
+        for i in range(4):
+            nc.sync.dma_start(
+                out=xt_sc[i:P:32, :].bitcast(I32).rearrange("q (g c) -> q g c", g=2),
+                in_=xts[i].bitcast(I32),
+            )
+        nc.sync.dma_start(out=we_raw[:].bitcast(I32), in_=we_words[0].bitcast(I32))
+        load_ws(0, 1)
+        nc.sync.dma_start(
+            out=xt_w[:].bitcast(I32).rearrange("p (g c) -> p g c", g=2),
+            in_=xt_words.rearrange("g p c -> p g c").bitcast(I32),
+        )
+        nc.sync.dma_start(offsets[:], offs)
+        wes = we_scales[0].rearrange("(q i) c -> i q c", i=4)
+        for i in range(4):
+            nc.scalar.dma_start(out=we_sc_raw[i:P:32, :].bitcast(I32), in_=wes[i].bitcast(I32))
+        xes = xe_scales[0].rearrange("(q i) c -> i q c", i=4)
+        for i in range(4):
+            nc.scalar.dma_start(out=xe_sc[i:P:32, :].bitcast(I32), in_=xes[i].bitcast(I32))
+
+        dwin = [held.tile([P, T], F32, name="dwin%d" % i) for i in range(2)]
+        for w in dwin:
+            nc.gpsimd.memset(w[:], 0.0)
+
+        we_w = held.tile([P, 2 * N], U8, name="we_w", align_bytes=64)
+        nc.vector.tensor_copy(
+            out=we_w[:].bitcast(U16).rearrange("p (r m) -> p r m", r=R),
+            in_=we_raw[:].bitcast(U16).rearrange("p (m r) -> p r m", r=R),
+        )
+
+        res_v = res.rearrange("(p r) t -> r p t", r=R)
+        res_t = {}
+
+        def load_res(r):
+            res_t[r] = ring.tile([P, T], F32, name="res%d" % r, tag="stage")
+            nc.sync.dma_start(out=res_t[r][:], in_=res_v[r])
+
+        ws_codes, ws_sc = [], []
+        for g in range(2):
+            grouped = held.tile([P, N * 4], BF16, name="ws_bf%d" % g, tag="ws_bf%d" % g, align_bytes=64)
+            gv = grouped[:].rearrange("p (r m j) -> p m r j", r=R, j=4)
+            for h in range(2):
+                nc.vector.tensor_copy(
+                    out=gv[:, h * 64 : (h + 1) * 64],
+                    in_=ws_raw[g, h][:].rearrange("p j (m r) -> p m r j", r=R),
+                )
+                if g == 0:
+                    load_ws(1, h)
+            codes = held.tile([P, N], U32, name="ws_codes%d" % g, align_bytes=64)
+            sc = held.tile([P, N], U8, name="ws_sc%d" % g, align_bytes=64)
+            if g == 0:
+                nc.vector.quantize_mx(out=codes[:].bitcast(FP8X4), scales=sc[:], in_=grouped[:])
+                xe_w = held.tile([P, 4 * J], U8, name="xe_w", tag="ws_bf0", align_bytes=64)
+                nc.sync.dma_start(
+                    out=xe_w[:].bitcast(I32), in_=xe_words[0].rearrange("p c t -> p (c t)").bitcast(I32)
+                )
+            else:
+                for c0, c1 in ((0, P), (P, 2 * P), (2 * P, 4 * P)):
+                    nc.vector.quantize_mx(
+                        out=codes[:, c0:c1].bitcast(FP8X4), scales=sc[:, c0:c1], in_=grouped[:, 4 * c0 : 4 * c1]
+                    )
+            ws_codes.append(codes)
+            ws_sc.append(sc)
+        load_res(0)
+        load_res(3)
+        we_sc = held.tile([P, N], U8, name="we_sc", align_bytes=64)
+        nc.vector.tensor_copy(
+            out=we_sc[:].rearrange("p (r m) -> p r m", r=R),
+            in_=we_sc_raw[:].rearrange("p (m r) -> p r m", r=R),
+        )
+
+        def u_pass(r, h, g, acc):
+            cols = slice(r * P, (r + 1) * P)
+            t0 = g * T + h * BANK
+            nc.tensor.matmul_mx(
+                out=acc[:],
+                lhsT=ws_codes[g][:, cols].bitcast(FP8X4),
+                lhsT_scale=ws_sc[g][:, cols],
+                rhs=xt_w[:, 2 * t0 : 2 * (t0 + BANK)].bitcast(FP4X4),
+                rhs_scale=xt_sc[:, t0 : t0 + BANK],
+                start=(g == 0),
+                stop=(g == 1),
+            )
+
+        def p_pass(r, acc):
+            nc.tensor.matmul_mx(
+                out=acc[:],
+                lhsT=we_w[:, 2 * r * P : 2 * (r + 1) * P].bitcast(FP4X4),
+                lhsT_scale=we_sc[:, r * P : (r + 1) * P],
+                rhs=xe_w[:].bitcast(FP8X4),
+                rhs_scale=xe_sc[:],
+                start=True,
+                stop=True,
+            )
+
+        u5 = [held.tile([P, T], F32, name="u5_%d" % r) for r in range(R)]
+        th = [held.tile([P, J], F32, name="th%d" % r) for r in range(R)]
+
+        def u_out(r, h, acc):
+            nc.scalar.activation(u5[r][:, h * BANK : (h + 1) * BANK], acc[:], ACT.Copy, scale=UP)
+
+        def tanh_out(r, acc):
+            nc.scalar.activation(th[r][:], acc[:], ACT.Tanh, scale=-1.0)
+
+        ub = {(r, h): bank(2 * r + h, "u%d%d" % (r, h)) for r in range(2) for h in range(2)}
+        for r in range(2):
+            for h in range(2):
+                u_pass(r, h, 0, ub[r, h])
+        for r in range(2):
+            for h in range(2):
+                u_pass(r, h, 1, ub[r, h])
+        u_out(0, 0, ub[0, 0])
+        nc.vector.tensor_scalar(u5[0][:, BANK:], ub[0, 1][:], UP, None, ALU.mult)
+        pb = [bank(4 + r, "p%d" % r) for r in range(R)]
+        p_pass(0, pb[0])
+        u_out(1, 0, ub[1, 0])
+        u_out(1, 1, ub[1, 1])
+        tanh_out(0, pb[0])
+        for r in range(2, 4):
+            for h in range(2):
+                ub[r, h] = bank(2 * (r - 2) + h, "u%d%d" % (r, h))
+                u_pass(r, h, 0, ub[r, h])
+                u_pass(r, h, 1, ub[r, h])
+            p_pass(r - 1, pb[r - 1])
+            for h in range(2):
+                u_out(r, h, ub[r, h])
+            tanh_out(r - 1, pb[r - 1])
+        p_pass(3, pb[3])
+        tanh_out(3, pb[3])
+
+        ug = {}
+
+        def gather(r):
+            ug[r] = ring.tile([P, J], F32, name="ug", tag="ug")
+            nc.vector.tensor_copy(ug[r][:], u5[r][:].indirect(offsets[:]))
+
+        def scatter(r):
+            nc.vector.tensor_tensor(dwin[r % 2][:].indirect(offsets[:]), ug[r][:], th[r][:], ALU.mult)
+
+        def turn_add(acc, h, src, first, last):
+            for c in range(4):
+                t0 = h * BANK + c * P
+                nc.tensor.matmul(
+                    acc[:, c * P : (c + 1) * P],
+                    src[:, t0 : t0 + P],
+                    ident[:],
+                    start=(first and c == 0),
+                    stop=(last and c == 3),
+                    is_transpose=True,
+                )
+
+        ab = {}
+
+        def pre_sum(r, b0, close):
+            for h in range(2):
+                ab[r, h] = bank(b0 + h, "a%d%d" % (r, h))
+                turn_add(ab[r, h], h, u5[r], True, False)
+                turn_add(ab[r, h], h, res_t[r], False, close)
+
+        def add_d(r):
+            for h in range(2):
+                turn_add(ab[r, h], h, dwin[r % 2], False, True)
+
+        yb = {}
+
+        def turn_back(r, b0):
+            turned = {}
+            for h in range(2):
+                turned[h] = ring.tile([P, BANK], F32, name="turned", tag="turned%d" % h)
+                nc.scalar.activation(turned[h][:], ab[r, h][:], ACT.Copy, scale=RES_W)
+            for h in range(2):
+                yb[r, h] = bank(b0 + h, "y%d%d" % (r, h))
+                for c in range(4):
+                    nc.tensor.transpose(yb[r, h][:, c * P : (c + 1) * P], turned[h][:, c * P : (c + 1) * P], ident[:])
+
+        out_v = out_0.rearrange("(p r) t -> p r t", r=R)
+        y01 = held.tile([P, 2, T], F32, name="y01")
+        y23 = [held.tile([P, 2, BANK], F32, name="y23_%d" % h) for h in range(2)]
+
+        def y_out(r):
+            for h in range(2):
+                if r < 2:
+                    nc.scalar.copy(y01[:, r, h * BANK : (h + 1) * BANK], yb[r, h][:])
+                else:
+                    nc.scalar.copy(y23[h][:, 0, :], yb[r, h][:])
+            if r < 2:
+                nc.sync.dma_start(out=out_v[:, r, :], in_=y01[:, r, :])
+
+        z = [held.tile([P, QUART * 4], BF16, name="z%d" % q, align_bytes=64) for q in range(4)]
+
+        def zview(q, pair):
+            return z[q][:].rearrange("p (t r) -> p t r", r=4)[:, :, 2 * pair : 2 * pair + 2]
+
+        gather(0)
+        gather(1)
+        pre_sum(0, 4, False)
+        load_res(1)
+        scatter(0)
+        pre_sum(3, 0, True)
+        load_res(2)
+        add_d(0)
+        turn_back(3, 2)
+        gather(2)
+        turn_back(0, 6)
+        pre_sum(1, 0, False)
+        scatter(1)
+        y_out(0)
+        add_d(1)
+        gather(3)
+        turn_back(1, 6)
+        pre_sum(2, 4, False)
+        scatter(2)
+        y_out(1)
+        for q in range(2):
+            nc.scalar.copy(zview(q, 0), y01[:, :, q * QUART : (q + 1) * QUART].rearrange("p r t -> p t r"))
+        add_d(2)
+        scatter(3)
+        turn_back(2, 0)
+        y_out(2)
+        for q in range(2, 4):
+            nc.scalar.copy(zview(q, 0), y01[:, :, q * QUART : (q + 1) * QUART].rearrange("p r t -> p t r"))
+
+        y_codes = held.tile([P, T], U32, name="y_codes", align_bytes=64)
+        y_sc = held.tile([P, T], U8, name="y_sc", align_bytes=64)
+        for q in range(4):
+            h, c0 = divmod(q * QUART, BANK)
+            nc.vector.scalar_tensor_tensor(
+                y23[h][:, 1, c0 : c0 + QUART],
+                dwin[1][:, q * QUART : (q + 1) * QUART],
+                RES_W,
+                yb[3, h][:, c0 : c0 + QUART],
+                ALU.mult,
+                ALU.add,
+            )
+        for h in range(2):
+            nc.sync.dma_start(out=out_v[:, 2:4, h * BANK : (h + 1) * BANK], in_=y23[h][:])
+        for q in range(4):
+            h, c0 = divmod(q * QUART, BANK)
+            src = y23[h][:, :, c0 : c0 + QUART].rearrange("p r t -> p t r")
+            if q < 2:
+                nc.scalar.copy(zview(q, 1), src)
+            else:
+                nc.vector.tensor_copy(zview(q, 1), src)
+        words_out = out_1[0].rearrange("p c t -> p (c t)").bitcast(I32)
+        for q in (0, 2, 3, 1):
+            cols = slice(q * QUART, (q + 1) * QUART)
+            nc.vector.quantize_mx(out=y_codes[:, cols].bitcast(FP8X4), scales=y_sc[:, cols], in_=z[q][:])
+        for h in (1, 0):
+            cols = slice(h * BANK, (h + 1) * BANK)
+            nc.sync.dma_start(out=words_out[:, cols], in_=y_codes[:, cols].bitcast(I32))
+        for q in range(4):
+            eng = nc.scalar if q % 2 else nc.sync
+            eng.dma_start(out=out_2[0][4 * q : 4 * q + 4, :].bitcast(I32), in_=y_sc[32 * q : 32 * q + 4, :].bitcast(I32))

@@ -24,6 +24,7 @@ HALVES = T // BANK
 QUART = 256
 RES_W = 0.2
 UP = 5.0
+M_VEC = 84
 
 
 def tile_moe_expert_scales_shared_answer_pl_kernel(
@@ -45,90 +46,83 @@ def tile_moe_expert_scales_shared_answer_pl_kernel(
         we_sc_raw = held.tile([P, N], U8, name="we_sc_raw", align_bytes=64)
         nc.vector.memset(xt_sc[:].bitcast(I32), 0)
         nc.vector.memset(we_sc_raw[:].bitcast(I32), 0)
-        nc.vector.memset(xe_sc[:].bitcast(I32), 0)
-
+        nc.gpsimd.memset(xe_sc[:].bitcast(I32), 0)
+        xes = xe_scales[0].rearrange("(q i) c -> i q c", i=4)
+        for i in range(4):
+            nc.gpsimd.dma_start(out=xe_sc[i:P:32, :].bitcast(I32), in_=xes[i].bitcast(I32))
         ident = held.tile([P, P], F32, name="ident")
         make_identity(nc, ident[:])
+
         we_raw = held.tile([P, 2 * N], U8, name="we_raw", align_bytes=64)
         ws_v = ws.rearrange("(g p j) n -> g p j n", g=2, j=4)
         ws_raw = {}
-        xt_w = held.tile([P, 2 * 2 * T], U8, name="xt_w", align_bytes=64)
 
-        def load_ws(g, h):
-            ws_raw[g, h] = ring.tile([P, 4, N // 2], F32, name="ws_raw%d%d" % (g, h), tag="stage")
-            nc.sync.dma_start(out=ws_raw[g, h][:], in_=ws_v[g][:, :, h * (N // 2) : (h + 1) * (N // 2)])
-
-        load_ws(0, 0)
+        xt_sc_in = held.tile([P, 2 * T], U8, name="xt_sc_in", align_bytes=64)
         xts = xt_scales.rearrange("g (q i) c -> i q g c", i=4)
         for i in range(4):
             nc.sync.dma_start(
-                out=xt_sc[i:P:32, :].bitcast(I32).rearrange("q (g c) -> q g c", g=2),
+                out=xt_sc_in[i:P:32, :].bitcast(I32).rearrange("q (g c) -> q g c", g=2),
                 in_=xts[i].bitcast(I32),
             )
-        nc.sync.dma_start(out=we_raw[:].bitcast(I32), in_=we_words[0].bitcast(I32))
-        load_ws(0, 1)
-        nc.sync.dma_start(
-            out=xt_w[:].bitcast(I32).rearrange("p (g c) -> p g c", g=2),
-            in_=xt_words.rearrange("g p c -> p g c").bitcast(I32),
-        )
-        nc.sync.dma_start(offsets[:], offs)
+        xt_all = held.tile([P, 2 * 2 * T], U8, name="xt_all", align_bytes=64)
+        for g in range(2):
+            ws_raw[g] = held.tile([P, 4, N], F32, name="ws_raw%d" % g)
+            nc.sync.dma_start(out=ws_raw[g][:], in_=ws_v[g])
+            if g == 0:
+                nc.sync.dma_start(out=we_raw[:].bitcast(I32), in_=we_words[0].bitcast(I32))
+                nc.sync.dma_start(
+                    out=xt_all[:].bitcast(I32).rearrange("p (g c) -> p g c", g=2),
+                    in_=xt_words.rearrange("g p c -> p g c").bitcast(I32),
+                )
         wes = we_scales[0].rearrange("(q i) c -> i q c", i=4)
         for i in range(4):
-            nc.scalar.dma_start(out=we_sc_raw[i:P:32, :].bitcast(I32), in_=wes[i].bitcast(I32))
-        xes = xe_scales[0].rearrange("(q i) c -> i q c", i=4)
-        for i in range(4):
-            nc.scalar.dma_start(out=xe_sc[i:P:32, :].bitcast(I32), in_=xes[i].bitcast(I32))
+            nc.sync.dma_start(out=we_sc_raw[i:P:32, :].bitcast(I32), in_=wes[i].bitcast(I32))
+        xe_w = held.tile([P, 4 * J], U8, name="xe_w", align_bytes=64)
+        nc.sync.dma_start(out=xe_w[:].bitcast(I32), in_=xe_words[0].rearrange("p c t -> p (c t)").bitcast(I32))
+        nc.sync.dma_start(offsets[:], offs)
+        res_v = res.rearrange("(p r) t -> r p t", r=R)
+        res_t = {}
+        for r in (0, 3, 1, 2):
+            res_t[r] = held.tile([P, T], F32, name="res%d" % r)
+            nc.sync.dma_start(out=res_t[r][:], in_=res_v[r])
 
         dwin = [held.tile([P, T], F32, name="dwin%d" % i) for i in range(2)]
         for w in dwin:
-            nc.gpsimd.memset(w[:], 0.0)
+            nc.vector.memset(w[:], 0.0)
 
+        for q in range(4):
+            rows = slice(32 * q, 32 * q + 4)
+            nc.vector.tensor_copy(out=xt_sc[rows, :].bitcast(I32), in_=xt_sc_in[rows, :].bitcast(I32))
+        ws_codes = [held.tile([P, N], U32, name="ws_codes%d" % g, align_bytes=64) for g in range(2)]
+        ws_sc = [held.tile([P, N], U8, name="ws_sc%d" % g, align_bytes=64) for g in range(2)]
+
+        def quantize_ws(g, c0, c1, src):
+            nc.vector.quantize_mx(out=ws_codes[g][:, c0:c1].bitcast(FP8X4), scales=ws_sc[g][:, c0:c1], in_=src)
+
+        bf0 = held.tile([P, N * 4], BF16, name="ws_bf0", align_bytes=64)
+        dst0 = bf0[:].rearrange("p (r m j) -> p m r j", r=R, j=4)
+        src0 = ws_raw[0][:].rearrange("p j (m r) -> p m r j", r=R)
+        nc.vector.tensor_copy(out=dst0[:, :M_VEC], in_=src0[:, :M_VEC])
+        nc.scalar.activation(dst0[:, M_VEC:], src0[:, M_VEC:], ACT.Copy)
+        quantize_ws(0, 0, N, bf0[:])
         we_w = held.tile([P, 2 * N], U8, name="we_w", align_bytes=64)
         nc.vector.tensor_copy(
             out=we_w[:].bitcast(U16).rearrange("p (r m) -> p r m", r=R),
             in_=we_raw[:].bitcast(U16).rearrange("p (m r) -> p r m", r=R),
         )
-
-        res_v = res.rearrange("(p r) t -> r p t", r=R)
-        res_t = {}
-
-        def load_res(r):
-            res_t[r] = ring.tile([P, T], F32, name="res%d" % r, tag="stage")
-            nc.sync.dma_start(out=res_t[r][:], in_=res_v[r])
-
-        ws_codes, ws_sc = [], []
-        for g in range(2):
-            grouped = held.tile([P, N * 4], BF16, name="ws_bf%d" % g, tag="ws_bf%d" % g, align_bytes=64)
-            gv = grouped[:].rearrange("p (r m j) -> p m r j", r=R, j=4)
-            for h in range(2):
-                nc.vector.tensor_copy(
-                    out=gv[:, h * 64 : (h + 1) * 64],
-                    in_=ws_raw[g, h][:].rearrange("p j (m r) -> p m r j", r=R),
-                )
-                if g == 0:
-                    load_ws(1, h)
-            codes = held.tile([P, N], U32, name="ws_codes%d" % g, align_bytes=64)
-            sc = held.tile([P, N], U8, name="ws_sc%d" % g, align_bytes=64)
-            if g == 0:
-                nc.vector.quantize_mx(out=codes[:].bitcast(FP8X4), scales=sc[:], in_=grouped[:])
-                xe_w = held.tile([P, 4 * J], U8, name="xe_w", tag="ws_bf0", align_bytes=64)
-                nc.sync.dma_start(
-                    out=xe_w[:].bitcast(I32), in_=xe_words[0].rearrange("p c t -> p (c t)").bitcast(I32)
-                )
-            else:
-                for c0, c1 in ((0, P), (P, 2 * P), (2 * P, 4 * P)):
-                    nc.vector.quantize_mx(
-                        out=codes[:, c0:c1].bitcast(FP8X4), scales=sc[:, c0:c1], in_=grouped[:, 4 * c0 : 4 * c1]
-                    )
-            ws_codes.append(codes)
-            ws_sc.append(sc)
-        load_res(0)
-        load_res(3)
         we_sc = held.tile([P, N], U8, name="we_sc", align_bytes=64)
         nc.vector.tensor_copy(
             out=we_sc[:].rearrange("p (r m) -> p r m", r=R),
             in_=we_sc_raw[:].rearrange("p (m r) -> p r m", r=R),
         )
+        src1 = ws_raw[1][:].rearrange("p j (m r) -> p m r j", r=R)
+        bf1 = [held.tile([P, P * 4], BF16, name="ws_bf1_%d" % r, align_bytes=64) for r in range(2)]
+        bf23 = held.tile([P, 2 * P * 4], BF16, name="ws_bf23", align_bytes=64)
+        nc.scalar.activation(bf23[:].rearrange("p (r m j) -> p m r j", r=2, j=4), src1[:, :, 2:4, :], ACT.Copy)
+        for r in range(2):
+            nc.vector.tensor_copy(out=bf1[r][:].rearrange("p (m j) -> p m j", j=4), in_=src1[:, :, r, :])
+            quantize_ws(1, r * P, (r + 1) * P, bf1[r][:])
+        quantize_ws(1, 2 * P, 4 * P, bf23[:])
 
         def u_pass(r, h, g, acc):
             cols = slice(r * P, (r + 1) * P)
@@ -137,7 +131,7 @@ def tile_moe_expert_scales_shared_answer_pl_kernel(
                 out=acc[:],
                 lhsT=ws_codes[g][:, cols].bitcast(FP8X4),
                 lhsT_scale=ws_sc[g][:, cols],
-                rhs=xt_w[:, 2 * t0 : 2 * (t0 + BANK)].bitcast(FP4X4),
+                rhs=xt_all[:, 2 * t0 : 2 * (t0 + BANK)].bitcast(FP4X4),
                 rhs_scale=xt_sc[:, t0 : t0 + BANK],
                 start=(g == 0),
                 stop=(g == 1),
@@ -158,7 +152,7 @@ def tile_moe_expert_scales_shared_answer_pl_kernel(
         th = [held.tile([P, J], F32, name="th%d" % r) for r in range(R)]
 
         def u_out(r, h, acc):
-            nc.scalar.activation(u5[r][:, h * BANK : (h + 1) * BANK], acc[:], ACT.Copy, scale=UP)
+            nc.scalar.activation(u5[r][:, h * BANK : (h + 1) * BANK], acc[:], ACT.Copy, scale=(1.0 if r == 2 else UP))
 
         def tanh_out(r, acc):
             nc.scalar.activation(th[r][:], acc[:], ACT.Tanh, scale=-1.0)
@@ -235,17 +229,21 @@ def tile_moe_expert_scales_shared_answer_pl_kernel(
                     nc.tensor.transpose(yb[r, h][:, c * P : (c + 1) * P], turned[h][:, c * P : (c + 1) * P], ident[:])
 
         out_v = out_0.rearrange("(p r) t -> p r t", r=R)
-        y01 = held.tile([P, 2, T], F32, name="y01")
-        y23 = [held.tile([P, 2, BANK], F32, name="y23_%d" % h) for h in range(2)]
+        SLOT = (1, 2, 0, 1)
+        ybuf = [held.tile([P, 3, BANK], F32, name="ybuf%d" % h) for h in range(2)]
+
+        def store_y(r, h):
+            (nc.scalar if r < 2 else nc.sync).dma_start(out=out_v[:, r, h * BANK : (h + 1) * BANK], in_=ybuf[h][:, SLOT[r], :])
 
         def y_out(r):
             for h in range(2):
-                if r < 2:
-                    nc.scalar.copy(y01[:, r, h * BANK : (h + 1) * BANK], yb[r, h][:])
-                else:
-                    nc.scalar.copy(y23[h][:, 0, :], yb[r, h][:])
-            if r < 2:
-                nc.sync.dma_start(out=out_v[:, r, :], in_=y01[:, r, :])
+                nc.scalar.copy(ybuf[h][:, SLOT[r], :], yb[r, h][:])
+                store_y(r, h)
+
+        def pair_src(q, pair):
+            h, c0 = divmod(q * QUART, BANK)
+            s0 = SLOT[2 * pair]
+            return ybuf[h][:, s0 : s0 + 2, c0 : c0 + QUART].rearrange("p r t -> p t r")
 
         z = [held.tile([P, QUART * 4], BF16, name="z%d" % q, align_bytes=64) for q in range(4)]
 
@@ -255,38 +253,36 @@ def tile_moe_expert_scales_shared_answer_pl_kernel(
         gather(0)
         gather(1)
         pre_sum(0, 4, False)
-        load_res(1)
         scatter(0)
         pre_sum(3, 0, True)
-        load_res(2)
         add_d(0)
-        turn_back(3, 2)
         gather(2)
         turn_back(0, 6)
-        pre_sum(1, 0, False)
+        turn_back(3, 2)
+        pre_sum(1, 4, False)
         scatter(1)
         y_out(0)
         add_d(1)
+        w2 = held.tile([P, T], F32, name="w2")
+        nc.vector.scalar_tensor_tensor(w2[:], res_t[2][:], RES_W, u5[2][:], ALU.mult, ALU.add)
         gather(3)
         turn_back(1, 6)
-        pre_sum(2, 4, False)
         scatter(2)
         y_out(1)
-        for q in range(2):
-            nc.scalar.copy(zview(q, 0), y01[:, :, q * QUART : (q + 1) * QUART].rearrange("p r t -> p t r"))
-        add_d(2)
+        for q in range(4):
+            nc.scalar.copy(zview(q, 0), pair_src(q, 0))
+        for h in range(2):
+            hs = slice(h * BANK, (h + 1) * BANK)
+            nc.vector.tensor_tensor(ybuf[h][:, SLOT[2], :], w2[:, hs], dwin[0][:, hs], ALU.add)
+            store_y(2, h)
         scatter(3)
-        turn_back(2, 0)
-        y_out(2)
-        for q in range(2, 4):
-            nc.scalar.copy(zview(q, 0), y01[:, :, q * QUART : (q + 1) * QUART].rearrange("p r t -> p t r"))
 
         y_codes = held.tile([P, T], U32, name="y_codes", align_bytes=64)
         y_sc = held.tile([P, T], U8, name="y_sc", align_bytes=64)
         for q in range(4):
             h, c0 = divmod(q * QUART, BANK)
             nc.vector.scalar_tensor_tensor(
-                y23[h][:, 1, c0 : c0 + QUART],
+                ybuf[h][:, SLOT[3], c0 : c0 + QUART],
                 dwin[1][:, q * QUART : (q + 1) * QUART],
                 RES_W,
                 yb[3, h][:, c0 : c0 + QUART],
@@ -294,10 +290,9 @@ def tile_moe_expert_scales_shared_answer_pl_kernel(
                 ALU.add,
             )
         for h in range(2):
-            nc.sync.dma_start(out=out_v[:, 2:4, h * BANK : (h + 1) * BANK], in_=y23[h][:])
+            store_y(3, h)
         for q in range(4):
-            h, c0 = divmod(q * QUART, BANK)
-            src = y23[h][:, :, c0 : c0 + QUART].rearrange("p r t -> p t r")
+            src = pair_src(q, 1)
             if q < 2:
                 nc.scalar.copy(zview(q, 1), src)
             else:

@@ -41,6 +41,8 @@ def tile_moe_expert_scales_shared_answer_pl_kernel(
 
         offsets = held.tile([P, J // 16], U16, name="offsets")
 
+        ident = held.tile([P, P], F32, name="ident")
+        make_identity(nc, ident[:])
         xt_sc = held.tile([P, 2 * T], U8, name="xt_sc", align_bytes=64)
         xe_sc = held.tile([P, J], U8, name="xe_sc", align_bytes=64)
         we_sc_raw = held.tile([P, N], U8, name="we_sc_raw", align_bytes=64)
@@ -50,8 +52,6 @@ def tile_moe_expert_scales_shared_answer_pl_kernel(
         xes = xe_scales[0].rearrange("(q i) c -> i q c", i=4)
         for i in range(4):
             nc.gpsimd.dma_start(out=xe_sc[i:P:32, :].bitcast(I32), in_=xes[i].bitcast(I32))
-        ident = held.tile([P, P], F32, name="ident")
-        make_identity(nc, ident[:])
 
         we_raw = held.tile([P, 2 * N], U8, name="we_raw", align_bytes=64)
         ws_v = ws.rearrange("(g p j) n -> g p j n", g=2, j=4)
@@ -59,16 +59,16 @@ def tile_moe_expert_scales_shared_answer_pl_kernel(
 
         xt_sc_in = held.tile([P, 2 * T], U8, name="xt_sc_in", align_bytes=64)
         xts = xt_scales.rearrange("g (q i) c -> i q g c", i=4)
-        for i in range(4):
-            nc.sync.dma_start(
-                out=xt_sc_in[i:P:32, :].bitcast(I32).rearrange("q (g c) -> q g c", g=2),
-                in_=xts[i].bitcast(I32),
-            )
         xt_all = held.tile([P, 2 * 2 * T], U8, name="xt_all", align_bytes=64)
         for g in range(2):
             ws_raw[g] = held.tile([P, 4, N], F32, name="ws_raw%d" % g)
             nc.sync.dma_start(out=ws_raw[g][:], in_=ws_v[g])
             if g == 0:
+                for i in range(4):
+                    nc.sync.dma_start(
+                        out=xt_sc_in[i:P:32, :].bitcast(I32).rearrange("q (g c) -> q g c", g=2),
+                        in_=xts[i].bitcast(I32),
+                    )
                 nc.sync.dma_start(out=we_raw[:].bitcast(I32), in_=we_words[0].bitcast(I32))
                 nc.sync.dma_start(
                     out=xt_all[:].bitcast(I32).rearrange("p (g c) -> p g c", g=2),
@@ -82,7 +82,7 @@ def tile_moe_expert_scales_shared_answer_pl_kernel(
         nc.sync.dma_start(offsets[:], offs)
         res_v = res.rearrange("(p r) t -> r p t", r=R)
         res_t = {}
-        for r in (0, 3, 1, 2):
+        for r in (0, 2, 1, 3):
             res_t[r] = held.tile([P, T], F32, name="res%d" % r)
             nc.sync.dma_start(out=res_t[r][:], in_=res_v[r])
 
@@ -152,7 +152,7 @@ def tile_moe_expert_scales_shared_answer_pl_kernel(
         th = [held.tile([P, J], F32, name="th%d" % r) for r in range(R)]
 
         def u_out(r, h, acc):
-            nc.scalar.activation(u5[r][:, h * BANK : (h + 1) * BANK], acc[:], ACT.Copy, scale=(1.0 if r == 2 else UP))
+            nc.scalar.activation(u5[r][:, h * BANK : (h + 1) * BANK], acc[:], ACT.Copy, scale=UP)
 
         def tanh_out(r, acc):
             nc.scalar.activation(th[r][:], acc[:], ACT.Tanh, scale=-1.0)
@@ -254,26 +254,29 @@ def tile_moe_expert_scales_shared_answer_pl_kernel(
         gather(1)
         pre_sum(0, 4, False)
         scatter(0)
-        pre_sum(3, 0, True)
+        pre_sum(2, 6, True)
+        turn_back(2, 0)
         add_d(0)
         gather(2)
-        turn_back(0, 6)
-        turn_back(3, 2)
-        pre_sum(1, 4, False)
+        pre_sum(1, 6, False)
+        turn_back(0, 2)
         scatter(1)
         y_out(0)
         add_d(1)
-        w2 = held.tile([P, T], F32, name="w2")
-        nc.vector.scalar_tensor_tensor(w2[:], res_t[2][:], RES_W, u5[2][:], ALU.mult, ALU.add)
         gather(3)
-        turn_back(1, 6)
+        turn_back(1, 2)
         scatter(2)
+        pre_sum(3, 6, True)
         y_out(1)
-        for q in range(4):
+        for q in range(2):
+            nc.scalar.copy(zview(q, 0), pair_src(q, 0))
+        turn_back(3, 4)
+        for q in range(2, 4):
             nc.scalar.copy(zview(q, 0), pair_src(q, 0))
         for h in range(2):
-            hs = slice(h * BANK, (h + 1) * BANK)
-            nc.vector.tensor_tensor(ybuf[h][:, SLOT[2], :], w2[:, hs], dwin[0][:, hs], ALU.add)
+            nc.vector.scalar_tensor_tensor(
+                ybuf[h][:, SLOT[2], :], dwin[0][:, h * BANK : (h + 1) * BANK], RES_W, yb[2, h][:], ALU.mult, ALU.add
+            )
             store_y(2, h)
         scatter(3)
 
@@ -301,8 +304,6 @@ def tile_moe_expert_scales_shared_answer_pl_kernel(
         for q in (0, 2, 3, 1):
             cols = slice(q * QUART, (q + 1) * QUART)
             nc.vector.quantize_mx(out=y_codes[:, cols].bitcast(FP8X4), scales=y_sc[:, cols], in_=z[q][:])
-        for h in (1, 0):
-            cols = slice(h * BANK, (h + 1) * BANK)
             nc.sync.dma_start(out=words_out[:, cols], in_=y_codes[:, cols].bitcast(I32))
         for q in range(4):
             eng = nc.scalar if q % 2 else nc.sync

from contextlib import ExitStack

import concourse.mybir as mybir
from concourse.masks import make_identity

K, L, T, J, N = 1024, 512, 1024, 512, 512
FLOPS = 2 * K * N * T + 2 * L * N * J

F32 = mybir.dt.float32
BF16 = mybir.dt.bfloat16
I32 = mybir.dt.int32
U32 = mybir.dt.uint32
U16 = mybir.dt.uint16
U8 = mybir.dt.uint8
FP8X4 = mybir.dt.float8_e4m3fn_x4
FP4X4 = mybir.dt.float4_e2m1fn_x4
ACT = mybir.ActivationFunctionType
ALU = mybir.AluOpType

P = 128
R = 4
BANK = 512
HALVES = T // BANK
QUART = 256
RES_W = 0.2
UP = 5.0
M_VEC = 84


def tile_moe_expert_scales_shared_answer_pl_kernel(
    tc, xt_words, xt_scales, ws, xe_words, xe_scales, we_words, we_scales, res, offs, out_0, out_1, out_2
):
    nc = tc.nc
    with ExitStack() as ctx:
        held = ctx.enter_context(tc.tile_pool(name="held", bufs=1))
        ring = ctx.enter_context(tc.tile_pool(name="ring", bufs=2))
        psum = ctx.enter_context(tc.psum_pool(name="psum", bufs=1))

        def bank(b, name):
            return psum.tile([P, BANK], F32, name=name, tag="bank%d" % b)

        offsets = held.tile([P, J // 16], U16, name="offsets")

        ident = held.tile([P, P], F32, name="ident")
        make_identity(nc, ident[:])
        xt_sc = held.tile([P, 2 * T], U8, name="xt_sc", align_bytes=64)
        xe_sc = held.tile([P, J], U8, name="xe_sc", align_bytes=64)
        we_sc_raw = held.tile([P, N], U8, name="we_sc_raw", align_bytes=64)
        nc.vector.memset(xt_sc[:].bitcast(I32), 0)
        nc.vector.memset(we_sc_raw[:].bitcast(I32), 0)
        nc.gpsimd.memset(xe_sc[:].bitcast(I32), 0)
        xes = xe_scales[0].rearrange("(q i) c -> i q c", i=4)
        for i in range(4):
            nc.gpsimd.dma_start(out=xe_sc[i:P:32, :].bitcast(I32), in_=xes[i].bitcast(I32))

        we_raw = held.tile([P, 2 * N], U8, name="we_raw", align_bytes=64)
        ws_v = ws.rearrange("(g p j) n -> g p j n", g=2, j=4)
        ws_raw = {}

        xt_sc_in = held.tile([P, 2 * T], U8, name="xt_sc_in", align_bytes=64)
        xts = xt_scales.rearrange("g (q i) c -> i q g c", i=4)
        xt_all = held.tile([P, 2 * 2 * T], U8, name="xt_all", align_bytes=64)
        for g in range(2):
            ws_raw[g] = held.tile([P, 4, N], F32, name="ws_raw%d" % g)
            nc.sync.dma_start(out=ws_raw[g][:], in_=ws_v[g])
            if g == 0:
                for i in range(4):
                    nc.sync.dma_start(
                        out=xt_sc_in[i:P:32, :].bitcast(I32).rearrange("q (g c) -> q g c", g=2),
                        in_=xts[i].bitcast(I32),
                    )
                nc.sync.dma_start(out=we_raw[:].bitcast(I32), in_=we_words[0].bitcast(I32))
                nc.sync.dma_start(
                    out=xt_all[:].bitcast(I32).rearrange("p (g c) -> p g c", g=2),
                    in_=xt_words.rearrange("g p c -> p g c").bitcast(I32),
                )
        wes = we_scales[0].rearrange("(q i) c -> i q c", i=4)
        for i in range(4):
            nc.sync.dma_start(out=we_sc_raw[i:P:32, :].bitcast(I32), in_=wes[i].bitcast(I32))
        xe_w = held.tile([P, 4 * J], U8, name="xe_w", align_bytes=64)
        nc.sync.dma_start(out=xe_w[:].bitcast(I32), in_=xe_words[0].rearrange("p c t -> p (c t)").bitcast(I32))
        nc.sync.dma_start(offsets[:], offs)
        res_v = res.rearrange("(p r) t -> r p t", r=R)
        res_t = {}
        for r in (0, 2, 1, 3):
            res_t[r] = held.tile([P, T], F32, name="res%d" % r)
            nc.sync.dma_start(out=res_t[r][:], in_=res_v[r])

        dwin = [held.tile([P, T], F32, name="dwin%d" % i) for i in range(2)]
        for w in dwin:
            nc.vector.memset(w[:], 0.0)

        for q in range(4):
            rows = slice(32 * q, 32 * q + 4)
            nc.vector.tensor_copy(out=xt_sc[rows, :].bitcast(I32), in_=xt_sc_in[rows, :].bitcast(I32))
        ws_codes = [held.tile([P, N], U32, name="ws_codes%d" % g, align_bytes=64) for g in range(2)]
        ws_sc = [held.tile([P, N], U8, name="ws_sc%d" % g, align_bytes=64) for g in range(2)]

        def quantize_ws(g, c0, c1, src):
            nc.vector.quantize_mx(out=ws_codes[g][:, c0:c1].bitcast(FP8X4), scales=ws_sc[g][:, c0:c1], in_=src)

        bf0 = held.tile([P, N * 4], BF16, name="ws_bf0", align_bytes=64)
        dst0 = bf0[:].rearrange("p (r m j) -> p m r j", r=R, j=4)
        src0 = ws_raw[0][:].rearrange("p j (m r) -> p m r j", r=R)
        nc.vector.tensor_copy(out=dst0[:, :M_VEC], in_=src0[:, :M_VEC])
        nc.scalar.activation(dst0[:, M_VEC:], src0[:, M_VEC:], ACT.Copy)
        quantize_ws(0, 0, N, bf0[:])
        we_w = held.tile([P, 2 * N], U8, name="we_w", align_bytes=64)
        nc.vector.tensor_copy(
            out=we_w[:].bitcast(U16).rearrange("p (r m) -> p r m", r=R),
            in_=we_raw[:].bitcast(U16).rearrange("p (m r) -> p r m", r=R),
        )
        we_sc = held.tile([P, N], U8, name="we_sc", align_bytes=64)
        nc.vector.tensor_copy(
            out=we_sc[:].rearrange("p (r m) -> p r m", r=R),
            in_=we_sc_raw[:].rearrange("p (m r) -> p r m", r=R),
        )
        src1 = ws_raw[1][:].rearrange("p j (m r) -> p m r j", r=R)
        bf1 = [held.tile([P, P * 4], BF16, name="ws_bf1_%d" % r, align_bytes=64) for r in range(2)]
        bf23 = held.tile([P, 2 * P * 4], BF16, name="ws_bf23", align_bytes=64)
        nc.scalar.activation(bf23[:].rearrange("p (r m j) -> p m r j", r=2, j=4), src1[:, :, 2:4, :], ACT.Copy)
        for r in range(2):
            nc.vector.tensor_copy(out=bf1[r][:].rearrange("p (m j) -> p m j", j=4), in_=src1[:, :, r, :])
            quantize_ws(1, r * P, (r + 1) * P, bf1[r][:])
        quantize_ws(1, 2 * P, 4 * P, bf23[:])

        def u_pass(r, h, g, acc):
            cols = slice(r * P, (r + 1) * P)
            t0 = g * T + h * BANK
            nc.tensor.matmul_mx(
                out=acc[:],
                lhsT=ws_codes[g][:, cols].bitcast(FP8X4),
                lhsT_scale=ws_sc[g][:, cols],
                rhs=xt_all[:, 2 * t0 : 2 * (t0 + BANK)].bitcast(FP4X4),
                rhs_scale=xt_sc[:, t0 : t0 + BANK],
                start=(g == 0),
                stop=(g == 1),
            )

        def p_pass(r, acc):
            nc.tensor.matmul_mx(
                out=acc[:],
                lhsT=we_w[:, 2 * r * P : 2 * (r + 1) * P].bitcast(FP4X4),
                lhsT_scale=we_sc[:, r * P : (r + 1) * P],
                rhs=xe_w[:].bitcast(FP8X4),
                rhs_scale=xe_sc[:],
                start=True,
                stop=True,
            )

        u5 = [held.tile([P, T], F32, name="u5_%d" % r) for r in range(R)]
        th = [held.tile([P, J], F32, name="th%d" % r) for r in range(R)]

        def u_out(r, h, acc):
            nc.scalar.activation(u5[r][:, h * BANK : (h + 1) * BANK], acc[:], ACT.Copy, scale=UP)

        def tanh_out(r, acc):
            nc.scalar.activation(th[r][:], acc[:], ACT.Tanh, scale=-1.0)

        ub = {(r, h): bank(2 * r + h, "u%d%d" % (r, h)) for r in range(2) for h in range(2)}
        for r in range(2):
            for h in range(2):
                u_pass(r, h, 0, ub[r, h])
        for r in range(2):
            for h in range(2):
                u_pass(r, h, 1, ub[r, h])
        u_out(0, 0, ub[0, 0])
        nc.vector.tensor_scalar(u5[0][:, BANK:], ub[0, 1][:], UP, None, ALU.mult)
        pb = [bank(4 + r, "p%d" % r) for r in range(R)]
        p_pass(0, pb[0])
        u_out(1, 0, ub[1, 0])
        u_out(1, 1, ub[1, 1])
        tanh_out(0, pb[0])
        for r in range(2, 4):
            for h in range(2):
                ub[r, h] = bank(2 * (r - 2) + h, "u%d%d" % (r, h))
                u_pass(r, h, 0, ub[r, h])
                u_pass(r, h, 1, ub[r, h])
            p_pass(r - 1, pb[r - 1])
            for h in range(2):
                u_out(r, h, ub[r, h])
            tanh_out(r - 1, pb[r - 1])
        p_pass(3, pb[3])
        tanh_out(3, pb[3])

        ug = {}

        def gather(r):
            ug[r] = ring.tile([P, J], F32, name="ug", tag="ug")
            nc.vector.tensor_copy(ug[r][:], u5[r][:].indirect(offsets[:]))

        def scatter(r):
            nc.vector.tensor_tensor(dwin[r % 2][:].indirect(offsets[:]), ug[r][:], th[r][:], ALU.mult)

        def turn_add(acc, h, src, first, last):
            for c in range(4):
                t0 = h * BANK + c * P
                nc.tensor.matmul(
                    acc[:, c * P : (c + 1) * P],
                    src[:, t0 : t0 + P],
                    ident[:],
                    start=(first and c == 0),
                    stop=(last and c == 3),
                    is_transpose=True,
                )

        ab = {}

        def pre_sum(r, b0, close):
            for h in range(2):
                ab[r, h] = bank(b0 + h, "a%d%d" % (r, h))
                turn_add(ab[r, h], h, u5[r], True, False)
                turn_add(ab[r, h], h, res_t[r], False, close)

        def add_d(r):
            for h in range(2):
                turn_add(ab[r, h], h, dwin[r % 2], False, True)

        yb = {}

        def turn_back(r, b0):
            turned = {}
            for h in range(2):
                turned[h] = ring.tile([P, BANK], F32, name="turned", tag="turned%d" % h)
                nc.scalar.activation(turned[h][:], ab[r, h][:], ACT.Copy, scale=RES_W)
            for h in range(2):
                yb[r, h] = bank(b0 + h, "y%d%d" % (r, h))
                for c in range(4):
                    nc.tensor.transpose(yb[r, h][:, c * P : (c + 1) * P], turned[h][:, c * P : (c + 1) * P], ident[:])

        out_v = out_0.rearrange("(p r) t -> p r t", r=R)
        SLOT = (1, 2, 0, 1)
        ybuf = [held.tile([P, 3, BANK], F32, name="ybuf%d" % h) for h in range(2)]

        def store_y(r, h):
            (nc.scalar if r < 2 else nc.sync).dma_start(out=out_v[:, r, h * BANK : (h + 1) * BANK], in_=ybuf[h][:, SLOT[r], :])

        def y_out(r):
            for h in range(2):
                nc.scalar.copy(ybuf[h][:, SLOT[r], :], yb[r, h][:])
                store_y(r, h)

        def pair_src(q, pair):
            h, c0 = divmod(q * QUART, BANK)
            s0 = SLOT[2 * pair]
            return ybuf[h][:, s0 : s0 + 2, c0 : c0 + QUART].rearrange("p r t -> p t r")

        z = [held.tile([P, QUART * 4], BF16, name="z%d" % q, align_bytes=64) for q in range(4)]

        def zview(q, pair):
            return z[q][:].rearrange("p (t r) -> p t r", r=4)[:, :, 2 * pair : 2 * pair + 2]

        gather(0)
        gather(1)
        pre_sum(0, 4, False)
        scatter(0)
        pre_sum(2, 6, True)
        turn_back(2, 0)
        add_d(0)
        gather(2)
        pre_sum(1, 6, False)
        turn_back(0, 2)
        scatter(1)
        y_out(0)
        add_d(1)
        gather(3)
        turn_back(1, 2)
        scatter(2)
        pre_sum(3, 6, True)
        y_out(1)
        for q in range(2):
            nc.scalar.copy(zview(q, 0), pair_src(q, 0))
        turn_back(3, 4)
        for q in range(2, 4):
            nc.scalar.copy(zview(q, 0), pair_src(q, 0))
        for h in range(2):
            nc.vector.scalar_tensor_tensor(
                ybuf[h][:, SLOT[2], :], dwin[0][:, h * BANK : (h + 1) * BANK], RES_W, yb[2, h][:], ALU.mult, ALU.add
            )
            store_y(2, h)
        scatter(3)

        y_codes = held.tile([P, T], U32, name="y_codes", align_bytes=64)
        y_sc = held.tile([P, T], U8, name="y_sc", align_bytes=64)
        for q in range(4):
            h, c0 = divmod(q * QUART, BANK)
            nc.vector.scalar_tensor_tensor(
                ybuf[h][:, SLOT[3], c0 : c0 + QUART],
                dwin[1][:, q * QUART : (q + 1) * QUART],
                RES_W,
                yb[3, h][:, c0 : c0 + QUART],
                ALU.mult,
                ALU.add,
            )
        for h in range(2):
            store_y(3, h)
        for q in range(4):
            src = pair_src(q, 1)
            if q < 2:
                nc.scalar.copy(zview(q, 1), src)
            else:
                nc.vector.tensor_copy(zview(q, 1), src)
        words_out = out_1[0].rearrange("p c t -> p (c t)").bitcast(I32)
        for q in (0, 2, 3, 1):
            cols = slice(q * QUART, (q + 1) * QUART)
            nc.vector.quantize_mx(out=y_codes[:, cols].bitcast(FP8X4), scales=y_sc[:, cols], in_=z[q][:])
            nc.sync.dma_start(out=words_out[:, cols], in_=y_codes[:, cols].bitcast(I32))
        for q in range(4):
            eng = nc.scalar if q % 2 else nc.sync
            eng.dma_start(out=out_2[0][4 * q : 4 * q + 4, :].bitcast(I32), in_=y_sc[32 * q : 32 * q + 4, :].bitcast(I32))
